import numpy as np
import ml_dtypes

BF16 = ml_dtypes.bfloat16


def bf(x):
    return np.asarray(x, np.float32).astype(BF16)


def f32(x):
    return np.asarray(x, np.float32)


def f64(x):
    return np.asarray(x).astype(np.float64)


def striped(idx):
    return np.concatenate([l.reshape(-1, 16).T for l in idx])


def rows(idx, k):
    return np.tile(np.repeat(idx, 16, axis=0), (k // (16 * 8), 1))


def look(tab, idx):
    return np.take_along_axis(f64(tab), rows(idx, len(tab)), axis=1)


K, S, D, V, N, M = 512, 2048, 3, 512, 1536, 512


def setup_inputs():
    return {"tab": f32(np.random.standard_normal((K, S))), "x0": f32(np.random.standard_normal((K, V))), "w": bf(np.random.standard_normal((K, M)) / np.sqrt(K)), "b": f32(0.5 * np.random.standard_normal((M, 1))), "offs": striped(np.stack([np.random.permutation(S)[:N] for _ in range(8)]))}


def reference(tab, x0, w, b, offs):
    idx = np.stack([g.T.reshape(-1) for g in np.split(offs, 8)])
    x = f64(x0)
    for d in range(D):
        x = np.minimum(x, look(tab, idx[:, d * V:(d + 1) * V]))
    y = f64(w).T @ x
    return np.maximum(y + f64(b), 0.0)

@@ -1,0 +1,63 @@
+import concourse.mybir as mybir
+
+F32, BF16, U16 = mybir.dt.float32, mybir.dt.bfloat16, mybir.dt.uint16
+MIN, MAX, ADD = mybir.AluOpType.min, mybir.AluOpType.max, mybir.AluOpType.add
+COPY, RELU = mybir.ActivationFunctionType.Copy, mybir.ActivationFunctionType.Relu
+
+P = 128
+K = 512
+S = 2048
+D = 3
+V = 512
+M = 512
+R = K // P
+MB = M // P
+C = V // 16
+
+FLOPS = 2 * K * M * V
+
+
+def tile_lookup_pool_min_relu_kernel(tc, tab, x0, w, b, offs, out):
+    nc = tc.nc
+    with (
+        tc.tile_pool(name="held", bufs=1) as held,
+        tc.tile_pool(name="running", bufs=4) as running,
+        tc.psum_pool(name="psum", bufs=1) as psum,
+    ):
+        offsets = held.tile([P, D * C], U16, name="offsets")
+        nc.sync.dma_start(offsets[:], offs)
+
+        tables, centres = [], []
+        for r in range(R):
+            table = held.tile([P, S], F32, name=f"table{r}")
+            nc.sync.dma_start(table[:], tab[r * P : (r + 1) * P, :])
+            centre = held.tile([P, V], F32, name=f"centre{r}")
+            nc.sync.dma_start(centre[:], x0[r * P : (r + 1) * P, :])
+            tables.append(table)
+            centres.append(centre)
+        weights = held.tile([P, R, M], BF16, name="weights")
+        nc.sync.dma_start(weights[:], w.rearrange("(r p) m -> p r m", p=P))
+        bias = held.tile([P, MB], F32, name="bias")
+        with nc.allow_non_contiguous_dma(reason="512 biases, one to a partition for each block of out's rows"):
+            nc.sync.dma_start(bias[:], b.rearrange("(m p) one -> p (m one)", p=P))
+
+        products = [psum.tile([P, V], F32, name=f"product{m}") for m in range(MB)]
+        for r in range(R):
+            low = centres[r]
+            for d in range(D):
+                lower = running.tile([P, V], F32, name="lower")
+                looked_up = tables[r][:].indirect(offsets[:, d * C : (d + 1) * C])
+                nc.vector.tensor_tensor(lower[:], looked_up, low[:], MIN)
+                low = lower
+            x = held.tile([P, V], BF16, name=f"x{r}")
+            nc.scalar.activation(x[:], low[:], COPY)
+            for m in range(MB):
+                nc.tensor.matmul(products[m][:], weights[:, r, m * P : (m + 1) * P], x[:], start=(r == 0), stop=(r == R - 1))
+
+        for m in range(MB):
+            result = held.tile([P, V], F32, name=f"result{m}")
+            if m % 2 == 0:
+                nc.scalar.activation(result[:], products[m][:], RELU, bias=bias[:, m : m + 1])
+            else:
+                nc.vector.tensor_scalar(result[:], products[m][:], bias[:, m : m + 1], 0.0, ADD, MAX)
+            nc.sync.dma_start(out[m * P : (m + 1) * P, :], result[:])

@@ -21,7 +21,7 @@ def tile_lookup_pool_min_relu_kernel(tc, tab, x0, w, b, offs, out):
     nc = tc.nc
     with (
         tc.tile_pool(name="held", bufs=1) as held,
-        tc.tile_pool(name="running", bufs=4) as running,
+        tc.tile_pool(name="running", bufs=8) as running,
         tc.psum_pool(name="psum", bufs=1) as psum,
     ):
         offsets = held.tile([P, D * C], U16, name="offsets")
@@ -42,17 +42,22 @@ def tile_lookup_pool_min_relu_kernel(tc, tab, x0, w, b, offs, out):
             nc.sync.dma_start(bias[:], b.rearrange("(m p) one -> p (m one)", p=P))
 
         products = [psum.tile([P, V], F32, name=f"product{m}") for m in range(MB)]
-        for r in range(R):
-            low = centres[r]
-            for d in range(D):
+        lows = list(centres)
+        for step in range(R + D - 1):
+            for r in range(R):
+                d = step - r
+                if d < 0 or d >= D:
+                    continue
                 lower = running.tile([P, V], F32, name="lower")
                 looked_up = tables[r][:].indirect(offsets[:, d * C : (d + 1) * C])
-                nc.vector.tensor_tensor(lower[:], looked_up, low[:], MIN)
-                low = lower
-            x = held.tile([P, V], BF16, name=f"x{r}")
-            nc.scalar.activation(x[:], low[:], COPY)
-            for m in range(MB):
-                nc.tensor.matmul(products[m][:], weights[:, r, m * P : (m + 1) * P], x[:], start=(r == 0), stop=(r == R - 1))
+                nc.vector.tensor_tensor(lower[:], looked_up, lows[r][:], MIN)
+                lows[r] = lower
+                if d == D - 1:
+                    x = held.tile([P, V], BF16, name=f"x{r}")
+                    nc.scalar.activation(x[:], lower[:], COPY)
+                    for m in range(MB):
+                        w_block = weights[:, r, m * P : (m + 1) * P]
+                        nc.tensor.matmul(products[m][:], w_block, x[:], start=(r == 0), stop=(r == R - 1))
 
         for m in range(MB):
             result = held.tile([P, V], F32, name=f"result{m}")

@@ -54,7 +54,10 @@ def tile_lookup_pool_min_relu_kernel(tc, tab, x0, w, b, offs, out):
                 lows[r] = lower
                 if d == D - 1:
                     x = held.tile([P, V], BF16, name=f"x{r}")
-                    nc.scalar.activation(x[:], lower[:], COPY)
+                    if r < R - 1:
+                        nc.scalar.activation(x[:], lower[:], COPY)
+                    else:
+                        nc.vector.tensor_copy(x[:], lower[:])
                     for m in range(MB):
                         w_block = weights[:, r, m * P : (m + 1) * P]
                         nc.tensor.matmul(products[m][:], w_block, x[:], start=(r == 0), stop=(r == R - 1))
@@ -63,6 +66,7 @@ def tile_lookup_pool_min_relu_kernel(tc, tab, x0, w, b, offs, out):
             result = held.tile([P, V], F32, name=f"result{m}")
             if m % 2 == 0:
                 nc.scalar.activation(result[:], products[m][:], RELU, bias=bias[:, m : m + 1])
+                nc.scalar.dma_start(out[m * P : (m + 1) * P, :], result[:])
             else:
                 nc.vector.tensor_scalar(result[:], products[m][:], bias[:, m : m + 1], 0.0, ADD, MAX)
-            nc.sync.dma_start(out[m * P : (m + 1) * P, :], result[:])
+                nc.sync.dma_start(out[m * P : (m + 1) * P, :], result[:])

import concourse.mybir as mybir

F32, BF16, U16 = mybir.dt.float32, mybir.dt.bfloat16, mybir.dt.uint16
MIN, MAX, ADD = mybir.AluOpType.min, mybir.AluOpType.max, mybir.AluOpType.add
COPY, RELU = mybir.ActivationFunctionType.Copy, mybir.ActivationFunctionType.Relu

P = 128
K = 512
S = 2048
D = 3
V = 512
M = 512
R = K // P
MB = M // P
C = V // 16

FLOPS = 2 * K * M * V


def tile_lookup_pool_min_relu_kernel(tc, tab, x0, w, b, offs, out):
    nc = tc.nc
    with (
        tc.tile_pool(name="held", bufs=1) as held,
        tc.tile_pool(name="running", bufs=8) as running,
        tc.psum_pool(name="psum", bufs=1) as psum,
    ):
        offsets = held.tile([P, D * C], U16, name="offsets")
        nc.sync.dma_start(offsets[:], offs)

        tables, centres = [], []
        for r in range(R):
            table = held.tile([P, S], F32, name=f"table{r}")
            nc.sync.dma_start(table[:], tab[r * P : (r + 1) * P, :])
            centre = held.tile([P, V], F32, name=f"centre{r}")
            nc.sync.dma_start(centre[:], x0[r * P : (r + 1) * P, :])
            tables.append(table)
            centres.append(centre)
        weights = held.tile([P, R, M], BF16, name="weights")
        nc.sync.dma_start(weights[:], w.rearrange("(r p) m -> p r m", p=P))
        bias = held.tile([P, MB], F32, name="bias")
        with nc.allow_non_contiguous_dma(reason="512 biases, one to a partition for each block of out's rows"):
            nc.sync.dma_start(bias[:], b.rearrange("(m p) one -> p (m one)", p=P))

        products = [psum.tile([P, V], F32, name=f"product{m}") for m in range(MB)]
        lows = list(centres)
        for step in range(R + D - 1):
            for r in range(R):
                d = step - r
                if d < 0 or d >= D:
                    continue
                lower = running.tile([P, V], F32, name="lower")
                looked_up = tables[r][:].indirect(offsets[:, d * C : (d + 1) * C])
                nc.vector.tensor_tensor(lower[:], looked_up, lows[r][:], MIN)
                lows[r] = lower
                if d == D - 1:
                    x = held.tile([P, V], BF16, name=f"x{r}")
                    if r < R - 1:
                        nc.scalar.activation(x[:], lower[:], COPY)
                    else:
                        nc.vector.tensor_copy(x[:], lower[:])
                    for m in range(MB):
                        w_block = weights[:, r, m * P : (m + 1) * P]
                        nc.tensor.matmul(products[m][:], w_block, x[:], start=(r == 0), stop=(r == R - 1))

        for m in range(MB):
            result = held.tile([P, V], F32, name=f"result{m}")
            if m % 2 == 0:
                nc.scalar.activation(result[:], products[m][:], RELU, bias=bias[:, m : m + 1])
                nc.scalar.dma_start(out[m * P : (m + 1) * P, :], result[:])
            else:
                nc.vector.tensor_scalar(result[:], products[m][:], bias[:, m : m + 1], 0.0, ADD, MAX)
                nc.sync.dma_start(out[m * P : (m + 1) * P, :], result[:])
